import numpy as np
import ml_dtypes


def mxq(x, axis, fmt="e4m3"):
    dtype, down = {"e4m3": (ml_dtypes.float8_e4m3fn, 7), "e5m2": (ml_dtypes.float8_e5m2, 14)}[fmt]
    v = np.moveaxis(np.asarray(x, np.float32).astype(ml_dtypes.bfloat16).astype(np.float64), axis, -1)
    blocks = v.reshape(v.shape[:-1] + (-1, 32))
    amax = np.abs(blocks).max(-1, keepdims=True)
    byte = np.maximum(np.where(amax > 0, np.frexp(amax)[1] - 1 + 127, 0) - down, 1)
    scale = np.exp2(byte - 127.0)
    codes = (blocks / scale).astype(np.float32).astype(dtype).astype(np.float64)
    return np.moveaxis((codes * scale).reshape(v.shape), -1, axis)


WIDE = False


def mx_kscale(k):
    if not WIDE:
        return np.ones(k)
    levels = np.array([10, -10, 5, -5, 0])
    if k % 512:
        return np.exp2(np.random.permutation(np.resize(levels, k // 32))).repeat(32)
    a = np.empty((k // 512, 16))
    for p in range(k // 512):
        a[p, :8] = np.random.permutation(np.resize(levels, 8))
        for g in range(8):
            far = levels[np.abs(levels - a[p, g]) >= 10]
            a[p, g + 8] = far[np.random.randint(len(far))]
    return np.exp2(a.ravel()).repeat(32)


def f64(x):
    return np.asarray(x).astype(np.float64)


def striped(idx):
    return np.tile(idx.reshape(-1, 16).T, (8, 1)).astype(np.uint16)


def unstriped(offs):
    return offs[:16].T.reshape(-1).astype(np.int64)


E2M1 = np.array([0.0, 0.5, 1.0, 1.5, 2.0, 3.0, 4.0, 6.0, -0.0, -0.5, -1.0, -1.5, -2.0, -3.0, -4.0, -6.0])


def pack_weight(w, fmt):
    k, n = w.shape
    w = f64(np.asarray(w, np.float32).astype(ml_dtypes.bfloat16)).reshape(k // 32, 32, n)
    amax = np.abs(w).max(1)
    if fmt == "e4m3":
        byte = np.frexp(amax)[1] - 1 + 127 - 7
    else:
        mant, ex = np.frexp(amax / 6.0)
        byte = np.where(mant > 0.5, ex, ex - 1) + 127
    byte = np.clip(np.where(amax > 0, byte, 1), 1, 254)
    scaled = (w * np.exp2(127.0 - byte)[:, None, :]).reshape(k, n).astype(np.float32)
    by_word = np.ascontiguousarray(scaled.reshape(k // 512, 128, 4, n).transpose(0, 1, 3, 2))
    if fmt == "e4m3":
        words = by_word.astype(ml_dtypes.float8_e4m3fn).view(np.uint8)
    else:
        c = by_word.astype(ml_dtypes.float4_e2m1fn).view(np.uint8) & 0xF
        words = (c[..., 0::2] | (c[..., 1::2] << 4)).reshape(k // 512, 128, 2 * n)
    return np.ascontiguousarray(words), np.ascontiguousarray(byte.astype(np.uint8).reshape(k // 512, 16, n))


def unpack_weight(words, scales, fmt):
    g, _, n = scales.shape
    words = np.ascontiguousarray(words).reshape(g, 128, n, -1)
    if fmt == "e4m3":
        vals = words.view(ml_dtypes.float8_e4m3fn).astype(np.float64)
    else:
        nib = np.empty((g, 128, n, 4), np.uint8)
        nib[..., 0::2] = words & 0xF
        nib[..., 1::2] = words >> 4
        vals = E2M1[nib]
    vals = vals * np.repeat(np.exp2(scales.astype(np.float64) - 127.0), 8, axis=1)[..., None]
    return vals.transpose(0, 1, 3, 2).reshape(g * 512, n)


def gelu(v):
    return 0.5 * v * (1.0 + np.tanh(np.sqrt(2.0 / np.pi) * (v + 0.044715 * v**3)))


K, T, S, H, T3, S2, P = 1024, 4096, 1024, 512, 2048, 1024, 512


def setup_inputs():
    n = np.random.standard_normal
    s = mx_kscale(K)[:, None]
    u = mx_kscale(H)[:, None]
    tab_words, tab_scales = pack_weight(n((K, T)) * s, "e4m3")
    tab2_words, tab2_scales = pack_weight(n((H, T3)) / u / np.sqrt(H), "e4m3")
    w1_words, w1_scales = pack_weight(1.4 * n((K, H)) / s / np.sqrt(K), "e2m1")
    return {
        "tab_words": tab_words, "tab_scales": tab_scales,
        "offs": striped(np.random.permutation(T)[:S]),
        "tab2_words": tab2_words, "tab2_scales": tab2_scales,
        "offs2": striped(np.random.permutation(T3)[:S2]),
        "pos1": striped(np.random.permutation(S)[:P]),
        "pos2": striped(np.random.permutation(S)[:P]),
        "w1_words": w1_words, "w1_scales": w1_scales,
        "w2": (0.52 * n((K, H)) / s / np.sqrt(K)).astype(np.float32),
        "w3": (0.8 * n((K, H)) / s / np.sqrt(K)).astype(np.float32),
        "gain": (np.exp(0.3 * n(H)) * u[:, 0]).astype(np.float32),
        "crowd": np.exp(0.4 * n(S2)).astype(np.float32),
    }


def reference(tab_words, tab_scales, offs, tab2_words, tab2_scales, offs2, pos1, pos2,
              w1_words, w1_scales, w2, w3, gain, crowd):
    v = unpack_weight(tab_words, tab_scales, "e4m3")[:, unstriped(offs)]
    v2 = unpack_weight(tab2_words, tab2_scales, "e4m3")[:, unstriped(offs2)]
    w1 = unpack_weight(w1_words, w1_scales, "e2m1")
    a = w1.T @ v
    b = mxq(f64(w2), 0, "e4m3").T @ v
    d = mxq(f64(w3), 0, "e4m3").T @ v
    h = f64(gain)[:, None] * (a * np.cos(b) + d)
    x1 = mxq(h[:, unstriped(pos1)], 0, "e4m3")
    x2 = mxq(np.abs(h[:, unstriped(pos2)]), 0, "e4m3")
    e1 = v2.T @ x1
    e2 = v2.T @ x2
    return f64(crowd)[:, None] * np.maximum(e1, e2)

@@ -1,0 +1,273 @@
+import math
+from contextlib import ExitStack
+
+import concourse.mybir as mybir
+
+K, T, S, H, T3, S2, NP = 1024, 4096, 1024, 512, 2048, 1024, 512
+FLOPS = 2 * (3 * K * H * S + 2 * H * S2 * NP)
+
+F32 = mybir.dt.float32
+BF16 = mybir.dt.bfloat16
+I32 = mybir.dt.int32
+U32 = mybir.dt.uint32
+U16 = mybir.dt.uint16
+U8 = mybir.dt.uint8
+FP8X4 = mybir.dt.float8_e4m3fn_x4
+FP4X4 = mybir.dt.float4_e2m1fn_x4
+ALU = mybir.AluOpType
+ACT = mybir.ActivationFunctionType
+
+P = 128
+PACK = 4
+KP = P * PACK
+BANK = 512
+HALF = 256
+
+
+def tile_list_next_stop_proposer_kernel(
+    tc, tab_words, tab_scales, offs, tab2_words, tab2_scales, offs2, pos1, pos2,
+    w1_words, w1_scales, w2, w3, gain, crowd, out,
+):
+    nc = tc.nc
+    with ExitStack() as ctx:
+        lists = ctx.enter_context(tc.tile_pool(name="lists", bufs=1))
+        keep = ctx.enter_context(tc.tile_pool(name="keep", bufs=1))
+        ring = ctx.enter_context(tc.tile_pool(name="ring", bufs=3))
+        psum = ctx.enter_context(tc.psum_pool(name="psum", bufs=8))
+
+        def held(shape, dtype, name, tag=None):
+            return keep.tile(shape, dtype, name=name, tag=tag or name, align_bytes=64)
+
+        idx = lists.tile([P, S // 16], U16, name="idx")
+        idx2 = lists.tile([P, S2 // 16], U16, name="idx2")
+        picks = [lists.tile([P, NP // 16], U16, name="pick%d" % i) for i in range(2)]
+
+        tab_s = held([P, T], U8, "tab_s")
+        tab2_s = held([P, T3], U8, "tab2_s")
+        w1_s_raw = held([P, 2, H], U8, "w1_s_raw")
+        v_s = [held([P, S], U8, "v_s%d" % a) for a in range(2)]
+        nc.vector.memset(tab2_s[:].bitcast(I32), 0)
+        nc.vector.memset(w1_s_raw[:].rearrange("p a c -> p (a c)").bitcast(I32), 0)
+        nc.vector.memset(tab_s[64:128, :].bitcast(I32), 0)
+        nc.vector.memset(tab_s[32:64, :].bitcast(I32), 0)
+        for a in range(2):
+            nc.vector.memset(v_s[a][:].bitcast(I32), 0)
+
+        tab = [held([P, T], U32, "tab%d" % a) for a in range(2)]
+        tab2 = held([P, T3], U32, "tab2")
+        w_raw = {}
+        for name, a in (("w2", 0), ("w2", 1), ("w3", 0)):
+            w_raw[name, a] = held([P, PACK, H], F32, "%s_raw%d" % (name, a))
+        w_raw["w3", 1] = held([P, PACK, H], F32, "w3_raw1", tag="h0_slot")
+        w1_raw = held([P, 2, 2 * H], U8, "w1_raw")
+        gain_sb = held([P, PACK], F32, "gain_sb")
+        crowd_sb = held([P, S2 // P], F32, "crowd_sb")
+
+        def load_w(name, w, a):
+            nc.sync.dma_start(
+                out=w_raw[name, a][:],
+                in_=w[a * KP : (a + 1) * KP, :].rearrange("(p j) c -> p j c", j=PACK),
+            )
+
+        def load_words(dst, words, a):
+            nc.sync.dma_start(
+                out=dst[:].bitcast(I32),
+                in_=words[a].rearrange("p n t -> p (n t)").bitcast(I32),
+            )
+
+        nc.sync.dma_start(idx[:], offs)
+        nc.sync.dma_start(
+            out=tab_s[0:32, :].bitcast(I32),
+            in_=tab_scales.rearrange("a q t -> (a q) t").bitcast(I32),
+        )
+        load_w("w2", w2, 0)
+        load_w("w2", w2, 1)
+        nc.sync.dma_start(idx2[:], offs2)
+        nc.sync.dma_start(
+            out=w1_raw[:].bitcast(I32), in_=w1_words.rearrange("a p c -> p a c").bitcast(I32)
+        )
+        nc.sync.dma_start(out=gain_sb[:], in_=gain.rearrange("(p t) -> p t", t=PACK))
+        load_words(tab[0], tab_words, 0)
+        for q in range(4):
+            nc.sync.dma_start(
+                out=tab2_s[32 * q : 32 * q + 4, :].bitcast(I32),
+                in_=tab2_scales[0, 4 * q : 4 * q + 4, :].bitcast(I32),
+            )
+        load_w("w3", w3, 0)
+        for q in range(4):
+            nc.sync.dma_start(
+                out=w1_s_raw[32 * q : 32 * q + 4, :, :].bitcast(I32),
+                in_=w1_scales[:, 4 * q : 4 * q + 4, :].rearrange("a r c -> r a c").bitcast(I32),
+            )
+        load_words(tab[1], tab_words, 1)
+        load_w("w3", w3, 1)
+        nc.sync.dma_start(picks[0][:], pos1)
+        nc.sync.dma_start(picks[1][:], pos2)
+        load_words(tab2, tab2_words, 0)
+        with nc.allow_non_contiguous_dma(reason="one factor a partition for each tile of rows"):
+            nc.sync.dma_start(out=crowd_sb[:], in_=crowd.rearrange("(i p) -> p i", p=P))
+
+        v_s_rows = held([P, S], U8, "v_s_rows")
+        nc.vector.tensor_copy(v_s_rows[:], tab_s[:].indirect(idx[:]))
+        for a in range(2):
+            for q in range(4):
+                row = 16 * a + 4 * q
+                nc.gpsimd.dma_start(
+                    out=v_s[a][32 * q : 32 * q + 4, :].bitcast(I32),
+                    in_=v_s_rows[row : row + 4, :].bitcast(I32),
+                )
+
+        w_bf = {}
+        w_c = {}
+        w_s = {}
+
+        def interleave_w(copy, name, a, tag=None):
+            w_bf[name, a] = held([P, PACK * H], BF16, "%s_bf%d" % (name, a), tag=tag)
+            copy(
+                w_bf[name, a][:].rearrange("p (t m j) -> p m t j", t=PACK, j=PACK),
+                w_raw[name, a][:].rearrange("p j (m t) -> p m t j", t=PACK),
+            )
+
+        def quantize_w(name, a):
+            w_c[name, a] = held([P, H], U32, "%s_c%d" % (name, a))
+            w_s[name, a] = held([P, H], U8, "%s_s%d" % (name, a))
+            nc.vector.quantize_mx(
+                out=w_c[name, a][:].bitcast(FP8X4), scales=w_s[name, a][:], in_=w_bf[name, a][:]
+            )
+
+        for name, a in (("w2", 0), ("w2", 1), ("w3", 0)):
+            interleave_w(nc.scalar.copy, name, a)
+
+        w1_c = held([P, 2, 2 * H], U8, "w1_c")
+        nc.vector.tensor_copy(
+            w1_c[:].rearrange("p a (t m b) -> p a t m b", t=PACK, b=2),
+            w1_raw[:].rearrange("p a (m t b) -> p a t m b", t=PACK, b=2),
+        )
+        quantize_w("w2", 0)
+        quantize_w("w2", 1)
+
+        v0 = held([P, S], U32, "v0")
+        nc.vector.tensor_copy(v0[:], tab[0][:].indirect(idx[:]))
+        v2_s = held([P, S2], U8, "v2_s")
+        nc.vector.tensor_copy(v2_s[:], tab2_s[:].indirect(idx2[:]))
+        w1_s = held([P, 2, H], U8, "w1_s")
+        nc.vector.tensor_copy(
+            w1_s[:].rearrange("p a (t m) -> p a t m", t=PACK),
+            w1_s_raw[:].rearrange("p a (m t) -> p a t m", t=PACK),
+        )
+        quantize_w("w3", 0)
+
+        v1 = [held([P, BANK], U32, "v1_%d" % c) for c in range(2)]
+        for c in range(2):
+            nc.vector.tensor_copy(v1[c][:], tab[1][:].indirect(idx[:, 32 * c : 32 * (c + 1)]))
+        interleave_w(nc.vector.tensor_copy, "w3", 1, tag="tab1")
+
+        def first_stage_product(name, t, c):
+            acc = psum.tile([P, BANK], F32, name="acc", tag="bank")
+            cols = slice(c * BANK, (c + 1) * BANK)
+            rows = slice(t * P, (t + 1) * P)
+            for a in range(2):
+                if name == "w1":
+                    lhsT = w1_c[:, a, 2 * t * P : 2 * (t + 1) * P].bitcast(FP4X4)
+                    lhsT_scale = w1_s[:, a, rows]
+                else:
+                    lhsT = w_c[name, a][:, rows].bitcast(FP8X4)
+                    lhsT_scale = w_s[name, a][:, rows]
+                rhs = v0[:, cols] if a == 0 else v1[c][:]
+                nc.tensor.matmul_mx(
+                    out=acc[:], lhsT=lhsT, lhsT_scale=lhsT_scale,
+                    rhs=rhs.bitcast(FP8X4), rhs_scale=v_s[a][:, cols],
+                    start=(a == 0), stop=(a == 1),
+                )
+            return acc
+
+        picked = [held([P, PACK, NP], F32, "picked%d" % i) for i in range(2)]
+        h_tags = {0: "h0_slot", 3: "h3_slot"}
+        h = {}
+
+        def pick(i, t, n0, n1):
+            nc.vector.tensor_copy(
+                picked[i][:, t, n0:n1], h[t][:].indirect(picks[i][:, n0 // 16 : n1 // 16])
+            )
+
+        for t in range(PACK):
+            h[t] = held([P, S], F32, "h%d" % t, tag=h_tags.get(t))
+            g = gain_sb[:, t : t + 1]
+            for c in range(2):
+                cols = slice(c * BANK, (c + 1) * BANK)
+                b = first_stage_product("w2", t, c)
+                a_sum = first_stage_product("w1", t, c)
+                b_abs = ring.tile([P, BANK], F32, name="b_abs")
+                nc.scalar.activation(b_abs[:], b[:], ACT.Abs)
+                cos_b = picked[c][:, (t - 1) % PACK, :]
+                nc.scalar.activation(cos_b, b_abs[:], ACT.Sin, bias=math.pi / 2, scale=-1.0)
+                nc.vector.scalar_tensor_tensor(
+                    out=h[t][:, cols], in0=cos_b, scalar=g, in1=a_sum[:], op0=ALU.mult, op1=ALU.mult
+                )
+                if t == 0 and c == 0:
+                    quantize_w("w3", 1)
+                if t > 0:
+                    pick(c, t - 1, 0, NP)
+                d = first_stage_product("w3", t, c)
+                nc.vector.scalar_tensor_tensor(
+                    out=h[t][:, cols], in0=d[:], scalar=g, in1=h[t][:, cols], op0=ALU.mult, op1=ALU.add
+                )
+
+        x_bf = {}
+        for n in range(2):
+            for i in range(2):
+                pick(i, PACK - 1, n * HALF, (n + 1) * HALF)
+                x_bf[i, n] = held([P, PACK * HALF], BF16, "x_bf%d_%d" % (i, n))
+                dst = x_bf[i, n][:].rearrange("p (c e t) -> p c t e", e=4, t=PACK)
+                src = picked[i][:, :, n * HALF : (n + 1) * HALF].rearrange("p t (c e) -> p c t e", e=4)
+                if i == 0:
+                    nc.scalar.copy(dst, src)
+                else:
+                    nc.scalar.activation(dst, src, ACT.Abs)
+
+        v2 = []
+        v2_tags = ("h3_slot", "x_bf1_0")
+        x_c = {}
+        x_s = {}
+        for n in range(2):
+            v2.append(held([P, BANK], U32, "v2_%d" % n, tag=v2_tags[n]))
+            nc.vector.tensor_copy(v2[n][:], tab2[:].indirect(idx2[:, 32 * n : 32 * (n + 1)]))
+            for i in range(2):
+                x_c[i, n] = held([P, HALF], U32, "x_c%d_%d" % (i, n))
+                x_s[i, n] = held([P, HALF], U8, "x_s%d_%d" % (i, n))
+                nc.vector.quantize_mx(
+                    out=x_c[i, n][:].bitcast(FP8X4), scales=x_s[i, n][:], in_=x_bf[i, n][:]
+                )
+
+        for n in range(2):
+            for k in range(4):
+                e = []
+                for i in range(2):
+                    acc = psum.tile([P, BANK], F32, name="acc", tag="bank")
+                    for r in range(2):
+                        rows = slice((2 * k + r) * P, (2 * k + r + 1) * P)
+                        part = slice((2 * (k % 2) + r) * P, (2 * (k % 2) + r + 1) * P)
+                        nc.tensor.matmul_mx(
+                            out=acc[:, r * HALF : (r + 1) * HALF],
+                            lhsT=v2[k // 2][:, part].bitcast(FP8X4), lhsT_scale=v2_s[:, rows],
+                            rhs=x_c[i, n][:].bitcast(FP8X4), rhs_scale=x_s[i, n][:],
+                            start=True, stop=True,
+                        )
+                    e.append(acc)
+                e1 = ring.tile([P, BANK], F32, name="e1")
+                nc.scalar.copy(e1[:], e[0][:])
+                larger = ring.tile([P, BANK], F32, name="larger")
+                nc.vector.tensor_tensor(larger[:], e[1][:], e1[:], ALU.max)
+                result = ring.tile([P, 2, HALF], F32, name="result", bufs=8)
+                for r in range(2):
+                    m = 2 * k + r
+                    nc.gpsimd.tensor_scalar(
+                        result[:, r, :], larger[:, r * HALF : (r + 1) * HALF],
+                        crowd_sb[:, m : m + 1], 0.0, ALU.mult, ALU.add,
+                    )
+                nc.sync.dma_start(
+                    out=out[2 * k * P : 2 * (k + 1) * P, n * HALF : (n + 1) * HALF].rearrange(
+                        "(r p) c -> p r c", p=P
+                    ),
+                    in_=result[:],
+                )

@@ -42,26 +42,27 @@ def tile_list_next_stop_proposer_kernel(
         idx2 = lists.tile([P, S2 // 16], U16, name="idx2")
         picks = [lists.tile([P, NP // 16], U16, name="pick%d" % i) for i in range(2)]
 
-        tab_s = held([P, T], U8, "tab_s")
+        warm = held([P, 2], F32, "warm")
+        nc.vector.memset(warm[:, 0:1], 0.0)
+        nc.scalar.activation(warm[:, 1:2], warm[:, 0:1], ACT.Sin)
+        tab_s = held([P, T], U8, "tab_s", tag="tab1")
         tab2_s = held([P, T3], U8, "tab2_s")
         w1_s_raw = held([P, 2, H], U8, "w1_s_raw")
         v_s = [held([P, S], U8, "v_s%d" % a) for a in range(2)]
-        nc.vector.memset(tab2_s[:].bitcast(I32), 0)
         nc.vector.memset(w1_s_raw[:].rearrange("p a c -> p (a c)").bitcast(I32), 0)
+        nc.vector.memset(tab2_s[:].bitcast(I32), 0)
         nc.vector.memset(tab_s[64:128, :].bitcast(I32), 0)
         nc.vector.memset(tab_s[32:64, :].bitcast(I32), 0)
         for a in range(2):
             nc.vector.memset(v_s[a][:].bitcast(I32), 0)
 
-        tab = [held([P, T], U32, "tab%d" % a) for a in range(2)]
-        tab2 = held([P, T3], U32, "tab2")
+        tab = [held([P, T], U32, "tab0")]
         w_raw = {}
-        for name, a in (("w2", 0), ("w2", 1), ("w3", 0)):
+        w_raw["w2", 0] = held([P, PACK, H], F32, "w2_raw0", tag="h0_slot")
+        for name, a in (("w2", 1), ("w3", 0)):
             w_raw[name, a] = held([P, PACK, H], F32, "%s_raw%d" % (name, a))
-        w_raw["w3", 1] = held([P, PACK, H], F32, "w3_raw1", tag="h0_slot")
         w1_raw = held([P, 2, 2 * H], U8, "w1_raw")
         gain_sb = held([P, PACK], F32, "gain_sb")
-        crowd_sb = held([P, S2 // P], F32, "crowd_sb")
 
         def load_w(name, w, a):
             nc.sync.dma_start(
@@ -95,20 +96,17 @@ def tile_list_next_stop_proposer_kernel(
             )
         load_w("w3", w3, 0)
         for q in range(4):
-            nc.sync.dma_start(
+            nc.gpsimd.dma_start(
                 out=w1_s_raw[32 * q : 32 * q + 4, :, :].bitcast(I32),
                 in_=w1_scales[:, 4 * q : 4 * q + 4, :].rearrange("a r c -> r a c").bitcast(I32),
             )
-        load_words(tab[1], tab_words, 1)
-        load_w("w3", w3, 1)
         nc.sync.dma_start(picks[0][:], pos1)
         nc.sync.dma_start(picks[1][:], pos2)
-        load_words(tab2, tab2_words, 0)
-        with nc.allow_non_contiguous_dma(reason="one factor a partition for each tile of rows"):
-            nc.sync.dma_start(out=crowd_sb[:], in_=crowd.rearrange("(i p) -> p i", p=P))
 
         v_s_rows = held([P, S], U8, "v_s_rows")
         nc.vector.tensor_copy(v_s_rows[:], tab_s[:].indirect(idx[:]))
+        tab.append(held([P, T], U32, "tab1"))
+        load_words(tab[1], tab_words, 1)
         for a in range(2):
             for q in range(4):
                 row = 16 * a + 4 * q
@@ -128,8 +126,8 @@ def tile_list_next_stop_proposer_kernel(
                 w_raw[name, a][:].rearrange("p j (m t) -> p m t j", t=PACK),
             )
 
-        def quantize_w(name, a):
-            w_c[name, a] = held([P, H], U32, "%s_c%d" % (name, a))
+        def quantize_w(name, a, tag=None):
+            w_c[name, a] = held([P, H], U32, "%s_c%d" % (name, a), tag=tag)
             w_s[name, a] = held([P, H], U8, "%s_s%d" % (name, a))
             nc.vector.quantize_mx(
                 out=w_c[name, a][:].bitcast(FP8X4), scales=w_s[name, a][:], in_=w_bf[name, a][:]
@@ -137,27 +135,34 @@ def tile_list_next_stop_proposer_kernel(
 
         for name, a in (("w2", 0), ("w2", 1), ("w3", 0)):
             interleave_w(nc.scalar.copy, name, a)
+        w_raw["w3", 1] = held([P, PACK, H], F32, "w3_raw1", tag="h0_slot")
+        load_w("w3", w3, 1)
+        tab2 = held([P, T3], U32, "tab2", tag="w2_raw1")
+        load_words(tab2, tab2_words, 0)
 
         w1_c = held([P, 2, 2 * H], U8, "w1_c")
         nc.vector.tensor_copy(
             w1_c[:].rearrange("p a (t m b) -> p a t m b", t=PACK, b=2),
             w1_raw[:].rearrange("p a (m t b) -> p a t m b", t=PACK, b=2),
         )
+        crowd_sb = held([P, S2 // P], F32, "crowd_sb", tag="w1_raw")
+        with nc.allow_non_contiguous_dma(reason="one factor a partition for each tile of rows"):
+            nc.sync.dma_start(out=crowd_sb[:], in_=crowd.rearrange("(i p) -> p i", p=P))
         quantize_w("w2", 0)
         quantize_w("w2", 1)
 
         v0 = held([P, S], U32, "v0")
         nc.vector.tensor_copy(v0[:], tab[0][:].indirect(idx[:]))
-        v2_s = held([P, S2], U8, "v2_s")
+        v2_s = held([P, S2], U8, "v2_s", tag="tab0")
         nc.vector.tensor_copy(v2_s[:], tab2_s[:].indirect(idx2[:]))
-        w1_s = held([P, 2, H], U8, "w1_s")
+        w1_s = held([P, 2, H], U8, "w1_s", tag="tab2_s")
         nc.vector.tensor_copy(
             w1_s[:].rearrange("p a (t m) -> p a t m", t=PACK),
             w1_s_raw[:].rearrange("p a (m t) -> p a t m", t=PACK),
         )
-        quantize_w("w3", 0)
+        quantize_w("w3", 0, tag="w1_s_raw")
 
-        v1 = [held([P, BANK], U32, "v1_%d" % c) for c in range(2)]
+        v1 = [held([P, BANK], U32, "v1_0", tag="w3_bf0"), held([P, BANK], U32, "v1_1")]
         for c in range(2):
             nc.vector.tensor_copy(v1[c][:], tab[1][:].indirect(idx[:, 32 * c : 32 * (c + 1)]))
         interleave_w(nc.vector.tensor_copy, "w3", 1, tag="tab1")
@@ -197,7 +202,10 @@ def tile_list_next_stop_proposer_kernel(
                 cols = slice(c * BANK, (c + 1) * BANK)
                 b = first_stage_product("w2", t, c)
                 a_sum = first_stage_product("w1", t, c)
-                b_abs = ring.tile([P, BANK], F32, name="b_abs")
+                if t < PACK - 1:
+                    b_abs = ring.tile([P, BANK], F32, name="b_abs")
+                else:
+                    b_abs = held([P, BANK], F32, "b_abs_last%d" % c, tag="x_bf%d" % c)
                 nc.scalar.activation(b_abs[:], b[:], ACT.Abs)
                 cos_b = picked[c][:, (t - 1) % PACK, :]
                 nc.scalar.activation(cos_b, b_abs[:], ACT.Sin, bias=math.pi / 2, scale=-1.0)
@@ -213,20 +221,25 @@ def tile_list_next_stop_proposer_kernel(
                     out=h[t][:, cols], in0=d[:], scalar=g, in1=h[t][:, cols], op0=ALU.mult, op1=ALU.add
                 )
 
-        x_bf = {}
+        x_bf = [held([P, PACK * NP], BF16, "x_bf%d" % i) for i in range(2)]
+
+        def interleave_x(i, t0, n0, n1):
+            dst = x_bf[i][:, PACK * n0 : PACK * n1].rearrange("p (n t) -> p n t", t=PACK)[:, :, t0 : t0 + 2]
+            src = picked[i][:, t0 : t0 + 2, n0:n1].rearrange("p t n -> p n t")
+            if i == 0:
+                nc.scalar.copy(dst, src)
+            else:
+                nc.scalar.activation(dst, src, ACT.Abs)
+
+        for i in range(2):
+            interleave_x(i, 0, 0, NP)
         for n in range(2):
             for i in range(2):
                 pick(i, PACK - 1, n * HALF, (n + 1) * HALF)
-                x_bf[i, n] = held([P, PACK * HALF], BF16, "x_bf%d_%d" % (i, n))
-                dst = x_bf[i, n][:].rearrange("p (c e t) -> p c t e", e=4, t=PACK)
-                src = picked[i][:, :, n * HALF : (n + 1) * HALF].rearrange("p t (c e) -> p c t e", e=4)
-                if i == 0:
-                    nc.scalar.copy(dst, src)
-                else:
-                    nc.scalar.activation(dst, src, ACT.Abs)
+                interleave_x(i, 2, n * HALF, (n + 1) * HALF)
 
         v2 = []
-        v2_tags = ("h3_slot", "x_bf1_0")
+        v2_tags = ("h3_slot", "picked1")
         x_c = {}
         x_s = {}
         for n in range(2):
@@ -236,7 +249,7 @@ def tile_list_next_stop_proposer_kernel(
                 x_c[i, n] = held([P, HALF], U32, "x_c%d_%d" % (i, n))
                 x_s[i, n] = held([P, HALF], U8, "x_s%d_%d" % (i, n))
                 nc.vector.quantize_mx(
-                    out=x_c[i, n][:].bitcast(FP8X4), scales=x_s[i, n][:], in_=x_bf[i, n][:]
+                    out=x_c[i, n][:].bitcast(FP8X4), scales=x_s[i, n][:], in_=x_bf[i][:, PACK * n * HALF : PACK * (n + 1) * HALF]
                 )
 
         for n in range(2):
@@ -259,12 +272,13 @@ def tile_list_next_stop_proposer_kernel(
                 larger = ring.tile([P, BANK], F32, name="larger")
                 nc.vector.tensor_tensor(larger[:], e[1][:], e1[:], ALU.max)
                 result = ring.tile([P, 2, HALF], F32, name="result", bufs=8)
-                for r in range(2):
-                    m = 2 * k + r
-                    nc.gpsimd.tensor_scalar(
-                        result[:, r, :], larger[:, r * HALF : (r + 1) * HALF],
-                        crowd_sb[:, m : m + 1], 0.0, ALU.mult, ALU.add,
-                    )
+                nc.gpsimd.tensor_scalar(
+                    result[:, 0, :], larger[:, :HALF],
+                    crowd_sb[:, 2 * k : 2 * k + 1], 0.0, ALU.mult, ALU.add,
+                )
+                nc.scalar.activation(
+                    result[:, 1, :], larger[:, HALF:], ACT.Copy, scale=crowd_sb[:, 2 * k + 1 : 2 * k + 2]
+                )
                 nc.sync.dma_start(
                     out=out[2 * k * P : 2 * (k + 1) * P, n * HALF : (n + 1) * HALF].rearrange(
                         "(r p) c -> p r c", p=P

@@ -33,7 +33,13 @@ def tile_list_next_stop_proposer_kernel(
         lists = ctx.enter_context(tc.tile_pool(name="lists", bufs=1))
         keep = ctx.enter_context(tc.tile_pool(name="keep", bufs=1))
         ring = ctx.enter_context(tc.tile_pool(name="ring", bufs=3))
-        psum = ctx.enter_context(tc.psum_pool(name="psum", bufs=8))
+        psum = ctx.enter_context(tc.psum_pool(name="psum", bufs=1))
+        taken = []
+
+        def next_bank():
+            taken.append(psum.tile([P, BANK], F32, name="bank%d" % (len(taken) % 8)))
+            return taken[-1]
+
 
         def held(shape, dtype, name, tag=None):
             return keep.tile(shape, dtype, name=name, tag=tag or name, align_bytes=64)
@@ -45,22 +51,20 @@ def tile_list_next_stop_proposer_kernel(
         warm = held([P, 2], F32, "warm")
         nc.vector.memset(warm[:, 0:1], 0.0)
         nc.scalar.activation(warm[:, 1:2], warm[:, 0:1], ACT.Sin)
-        tab_s = held([P, T], U8, "tab_s", tag="tab1")
+        tab_s = held([P, T], U8, "tab_s")
         tab2_s = held([P, T3], U8, "tab2_s")
         w1_s_raw = held([P, 2, H], U8, "w1_s_raw")
-        v_s = [held([P, S], U8, "v_s%d" % a) for a in range(2)]
+        v_s = [held([P, S], U8, "v_s0")]
         nc.vector.memset(w1_s_raw[:].rearrange("p a c -> p (a c)").bitcast(I32), 0)
-        nc.vector.memset(tab2_s[:].bitcast(I32), 0)
-        nc.vector.memset(tab_s[64:128, :].bitcast(I32), 0)
-        nc.vector.memset(tab_s[32:64, :].bitcast(I32), 0)
-        for a in range(2):
-            nc.vector.memset(v_s[a][:].bitcast(I32), 0)
+        for rows in (slice(0, 16), slice(32, 64), slice(64, 112)):
+            nc.vector.memset(tab_s[rows, :].bitcast(I32), 0)
+        nc.vector.memset(tab2_s[0:112, :].bitcast(I32), 0)
+        nc.vector.memset(v_s[0][:].bitcast(I32), 0)
 
         tab = [held([P, T], U32, "tab0")]
         w_raw = {}
-        w_raw["w2", 0] = held([P, PACK, H], F32, "w2_raw0", tag="h0_slot")
-        for name, a in (("w2", 1), ("w3", 0)):
-            w_raw[name, a] = held([P, PACK, H], F32, "%s_raw%d" % (name, a))
+        w_raw["w2", 0] = held([P, PACK, H], F32, "w2_raw0", tag="tab1")
+        w_raw["w2", 1] = held([P, PACK, H], F32, "w2_raw1", tag="h0_slot")
         w1_raw = held([P, 2, 2 * H], U8, "w1_raw")
         gain_sb = held([P, PACK], F32, "gain_sb")
 
@@ -77,43 +81,44 @@ def tile_list_next_stop_proposer_kernel(
             )
 
         nc.sync.dma_start(idx[:], offs)
-        nc.sync.dma_start(
-            out=tab_s[0:32, :].bitcast(I32),
-            in_=tab_scales.rearrange("a q t -> (a q) t").bitcast(I32),
-        )
+        scale_home = (16, 112)
+        for a in range(2):
+            nc.sync.dma_start(
+                out=tab_s[scale_home[a] : scale_home[a] + 16, :].bitcast(I32),
+                in_=tab_scales[a].bitcast(I32),
+            )
         load_w("w2", w2, 0)
-        load_w("w2", w2, 1)
         nc.sync.dma_start(idx2[:], offs2)
+        nc.sync.dma_start(out=tab2_s[112:128, :].bitcast(I32), in_=tab2_scales[0].bitcast(I32))
+        nc.sync.dma_start(picks[0][:], pos1)
+        nc.sync.dma_start(picks[1][:], pos2)
+        load_w("w2", w2, 1)
         nc.sync.dma_start(
             out=w1_raw[:].bitcast(I32), in_=w1_words.rearrange("a p c -> p a c").bitcast(I32)
         )
         nc.sync.dma_start(out=gain_sb[:], in_=gain.rearrange("(p t) -> p t", t=PACK))
         load_words(tab[0], tab_words, 0)
         for q in range(4):
-            nc.sync.dma_start(
-                out=tab2_s[32 * q : 32 * q + 4, :].bitcast(I32),
-                in_=tab2_scales[0, 4 * q : 4 * q + 4, :].bitcast(I32),
-            )
-        load_w("w3", w3, 0)
-        for q in range(4):
             nc.gpsimd.dma_start(
                 out=w1_s_raw[32 * q : 32 * q + 4, :, :].bitcast(I32),
                 in_=w1_scales[:, 4 * q : 4 * q + 4, :].rearrange("a r c -> r a c").bitcast(I32),
             )
-        nc.sync.dma_start(picks[0][:], pos1)
-        nc.sync.dma_start(picks[1][:], pos2)
 
         v_s_rows = held([P, S], U8, "v_s_rows")
         nc.vector.tensor_copy(v_s_rows[:], tab_s[:].indirect(idx[:]))
-        tab.append(held([P, T], U32, "tab1"))
-        load_words(tab[1], tab_words, 1)
-        for a in range(2):
+        w_raw["w3", 0] = held([P, PACK, H], F32, "w3_raw0", tag="tab_s")
+        load_w("w3", w3, 0)
+
+        def move_scale_rows(plane, rows, first):
             for q in range(4):
-                row = 16 * a + 4 * q
-                nc.gpsimd.dma_start(
-                    out=v_s[a][32 * q : 32 * q + 4, :].bitcast(I32),
-                    in_=v_s_rows[row : row + 4, :].bitcast(I32),
+                nc.sync.dma_start(
+                    out=plane[32 * q : 32 * q + 4, :].bitcast(I32),
+                    in_=rows[first + 4 * q : first + 4 * q + 4, :].bitcast(I32),
                 )
+
+        move_scale_rows(v_s[0], v_s_rows, scale_home[0])
+        v2_s_rows = held([P, S2], U8, "v2_s_rows")
+        nc.vector.tensor_copy(v2_s_rows[:], tab2_s[:].indirect(idx2[:]))
 
         w_bf = {}
         w_c = {}
@@ -133,34 +138,39 @@ def tile_list_next_stop_proposer_kernel(
                 out=w_c[name, a][:].bitcast(FP8X4), scales=w_s[name, a][:], in_=w_bf[name, a][:]
             )
 
-        for name, a in (("w2", 0), ("w2", 1), ("w3", 0)):
-            interleave_w(nc.scalar.copy, name, a)
+        interleave_w(nc.scalar.copy, "w2", 0)
+        tab.append(held([P, T], U32, "tab1"))
+        load_words(tab[1], tab_words, 1)
+        quantize_w("w2", 0)
+        v_s.append(held([P, S], U8, "v_s1", tag="w2_bf0"))
+        nc.vector.memset(v_s[1][:].bitcast(I32), 0)
+        move_scale_rows(v_s[1], v_s_rows, scale_home[1])
+
+        interleave_w(nc.scalar.copy, "w2", 1)
         w_raw["w3", 1] = held([P, PACK, H], F32, "w3_raw1", tag="h0_slot")
         load_w("w3", w3, 1)
-        tab2 = held([P, T3], U32, "tab2", tag="w2_raw1")
+        interleave_w(nc.scalar.copy, "w3", 0)
+        tab2 = held([P, T3], U32, "tab2", tag="tab_s")
         load_words(tab2, tab2_words, 0)
 
         w1_c = held([P, 2, 2 * H], U8, "w1_c")
         nc.vector.tensor_copy(
-            w1_c[:].rearrange("p a (t m b) -> p a t m b", t=PACK, b=2),
-            w1_raw[:].rearrange("p a (m t b) -> p a t m b", t=PACK, b=2),
+            w1_c[:].bitcast(U16).rearrange("p a (t m) -> p a t m", t=PACK),
+            w1_raw[:].bitcast(U16).rearrange("p a (m t) -> p a t m", t=PACK),
         )
-        crowd_sb = held([P, S2 // P], F32, "crowd_sb", tag="w1_raw")
-        with nc.allow_non_contiguous_dma(reason="one factor a partition for each tile of rows"):
-            nc.sync.dma_start(out=crowd_sb[:], in_=crowd.rearrange("(i p) -> p i", p=P))
-        quantize_w("w2", 0)
         quantize_w("w2", 1)
 
         v0 = held([P, S], U32, "v0")
         nc.vector.tensor_copy(v0[:], tab[0][:].indirect(idx[:]))
-        v2_s = held([P, S2], U8, "v2_s", tag="tab0")
-        nc.vector.tensor_copy(v2_s[:], tab2_s[:].indirect(idx2[:]))
-        w1_s = held([P, 2, H], U8, "w1_s", tag="tab2_s")
+        w1_s = held([P, 2, H], U8, "w1_s", tag="tab0")
         nc.vector.tensor_copy(
             w1_s[:].rearrange("p a (t m) -> p a t m", t=PACK),
             w1_s_raw[:].rearrange("p a (m t) -> p a t m", t=PACK),
         )
-        quantize_w("w3", 0, tag="w1_s_raw")
+        v2_s = held([P, S2], U8, "v2_s", tag="w1_s_raw")
+        nc.vector.memset(v2_s[:].bitcast(I32), 0)
+        move_scale_rows(v2_s, v2_s_rows, 112)
+        quantize_w("w3", 0)
 
         v1 = [held([P, BANK], U32, "v1_0", tag="w3_bf0"), held([P, BANK], U32, "v1_1")]
         for c in range(2):
@@ -168,7 +178,7 @@ def tile_list_next_stop_proposer_kernel(
         interleave_w(nc.vector.tensor_copy, "w3", 1, tag="tab1")
 
         def first_stage_product(name, t, c):
-            acc = psum.tile([P, BANK], F32, name="acc", tag="bank")
+            acc = next_bank()
             cols = slice(c * BANK, (c + 1) * BANK)
             rows = slice(t * P, (t + 1) * P)
             for a in range(2):
@@ -190,98 +200,99 @@ def tile_list_next_stop_proposer_kernel(
         h_tags = {0: "h0_slot", 3: "h3_slot"}
         h = {}
 
-        def pick(i, t, n0, n1):
-            nc.vector.tensor_copy(
-                picked[i][:, t, n0:n1], h[t][:].indirect(picks[i][:, n0 // 16 : n1 // 16])
+        def pick(i, t):
+            nc.vector.tensor_copy(picked[i][:, t, :], h[t][:].indirect(picks[i][:]))
+
+        def cosine_term(t, c):
+            b = first_stage_product("w2", t, c)
+            a_sum = first_stage_product("w1", t, c)
+            if t < PACK - 1:
+                b_abs = ring.tile([P, BANK], F32, name="b_abs")
+            else:
+                b_abs = held([P, BANK], F32, "b_abs_last%d" % c, tag="x_bf%d" % c)
+            nc.scalar.activation(b_abs[:], b[:], ACT.Abs)
+            cos_b = picked[c][:, (t - 1) % PACK, :]
+            nc.scalar.activation(cos_b, b_abs[:], ACT.Sin, bias=math.pi / 2, scale=-1.0)
+            nc.vector.scalar_tensor_tensor(
+                out=h[t][:, c * BANK : (c + 1) * BANK], in0=cos_b, scalar=gain_sb[:, t : t + 1],
+                in1=a_sum[:], op0=ALU.mult, op1=ALU.mult,
             )
 
-        for t in range(PACK):
+        def add_third_product(t, c):
+            d = first_stage_product("w3", t, c)
+            part = h[t][:, c * BANK : (c + 1) * BANK]
+            nc.vector.scalar_tensor_tensor(
+                out=part, in0=d[:], scalar=gain_sb[:, t : t + 1], in1=part, op0=ALU.mult, op1=ALU.add
+            )
+
+        h[0] = held([P, S], F32, "h0", tag=h_tags[0])
+        quantize_w("w3", 1)
+        cosine_term(0, 0)
+        cosine_term(0, 1)
+        add_third_product(0, 0)
+        add_third_product(0, 1)
+        crowd_sb = held([P, S2 // P], F32, "crowd_sb", tag="tab1")
+        with nc.allow_non_contiguous_dma(reason="one factor a partition for each tile of rows"):
+            nc.sync.dma_start(out=crowd_sb[:], in_=crowd.rearrange("(i p) -> p i", p=P))
+        for t in range(1, PACK):
             h[t] = held([P, S], F32, "h%d" % t, tag=h_tags.get(t))
-            g = gain_sb[:, t : t + 1]
             for c in range(2):
-                cols = slice(c * BANK, (c + 1) * BANK)
-                b = first_stage_product("w2", t, c)
-                a_sum = first_stage_product("w1", t, c)
-                if t < PACK - 1:
-                    b_abs = ring.tile([P, BANK], F32, name="b_abs")
-                else:
-                    b_abs = held([P, BANK], F32, "b_abs_last%d" % c, tag="x_bf%d" % c)
-                nc.scalar.activation(b_abs[:], b[:], ACT.Abs)
-                cos_b = picked[c][:, (t - 1) % PACK, :]
-                nc.scalar.activation(cos_b, b_abs[:], ACT.Sin, bias=math.pi / 2, scale=-1.0)
-                nc.vector.scalar_tensor_tensor(
-                    out=h[t][:, cols], in0=cos_b, scalar=g, in1=a_sum[:], op0=ALU.mult, op1=ALU.mult
-                )
-                if t == 0 and c == 0:
-                    quantize_w("w3", 1)
-                if t > 0:
-                    pick(c, t - 1, 0, NP)
-                d = first_stage_product("w3", t, c)
-                nc.vector.scalar_tensor_tensor(
-                    out=h[t][:, cols], in0=d[:], scalar=g, in1=h[t][:, cols], op0=ALU.mult, op1=ALU.add
-                )
+                cosine_term(t, c)
+                pick(c, t - 1)
+                add_third_product(t, c)
 
         x_bf = [held([P, PACK * NP], BF16, "x_bf%d" % i) for i in range(2)]
 
-        def interleave_x(i, t0, n0, n1):
-            dst = x_bf[i][:, PACK * n0 : PACK * n1].rearrange("p (n t) -> p n t", t=PACK)[:, :, t0 : t0 + 2]
-            src = picked[i][:, t0 : t0 + 2, n0:n1].rearrange("p t n -> p n t")
+        def interleave_x(i, t0):
+            dst = x_bf[i][:].rearrange("p (n t) -> p n t", t=PACK)[:, :, t0 : t0 + 2]
+            src = picked[i][:, t0 : t0 + 2, :].rearrange("p t n -> p n t")
             if i == 0:
                 nc.scalar.copy(dst, src)
             else:
                 nc.scalar.activation(dst, src, ACT.Abs)
 
         for i in range(2):
-            interleave_x(i, 0, 0, NP)
-        for n in range(2):
-            for i in range(2):
-                pick(i, PACK - 1, n * HALF, (n + 1) * HALF)
-                interleave_x(i, 2, n * HALF, (n + 1) * HALF)
+            interleave_x(i, 0)
+        for i in range(2):
+            pick(i, PACK - 1)
+            interleave_x(i, 2)
 
-        v2 = []
-        v2_tags = ("h3_slot", "picked1")
-        x_c = {}
-        x_s = {}
-        for n in range(2):
-            v2.append(held([P, BANK], U32, "v2_%d" % n, tag=v2_tags[n]))
-            nc.vector.tensor_copy(v2[n][:], tab2[:].indirect(idx2[:, 32 * n : 32 * (n + 1)]))
-            for i in range(2):
-                x_c[i, n] = held([P, HALF], U32, "x_c%d_%d" % (i, n))
-                x_s[i, n] = held([P, HALF], U8, "x_s%d_%d" % (i, n))
-                nc.vector.quantize_mx(
-                    out=x_c[i, n][:].bitcast(FP8X4), scales=x_s[i, n][:], in_=x_bf[i][:, PACK * n * HALF : PACK * (n + 1) * HALF]
-                )
+        def gather_exhibits(half, tag):
+            words = held([P, BANK], U32, "v2_%d" % half, tag=tag)
+            nc.vector.tensor_copy(words[:], tab2[:].indirect(idx2[:, 32 * half : 32 * (half + 1)]))
+            return words
 
-        for n in range(2):
-            for k in range(4):
-                e = []
-                for i in range(2):
-                    acc = psum.tile([P, BANK], F32, name="acc", tag="bank")
-                    for r in range(2):
-                        rows = slice((2 * k + r) * P, (2 * k + r + 1) * P)
-                        part = slice((2 * (k % 2) + r) * P, (2 * (k % 2) + r + 1) * P)
-                        nc.tensor.matmul_mx(
-                            out=acc[:, r * HALF : (r + 1) * HALF],
-                            lhsT=v2[k // 2][:, part].bitcast(FP8X4), lhsT_scale=v2_s[:, rows],
-                            rhs=x_c[i, n][:].bitcast(FP8X4), rhs_scale=x_s[i, n][:],
-                            start=True, stop=True,
-                        )
-                    e.append(acc)
-                e1 = ring.tile([P, BANK], F32, name="e1")
-                nc.scalar.copy(e1[:], e[0][:])
-                larger = ring.tile([P, BANK], F32, name="larger")
-                nc.vector.tensor_tensor(larger[:], e[1][:], e1[:], ALU.max)
-                result = ring.tile([P, 2, HALF], F32, name="result", bufs=8)
-                nc.gpsimd.tensor_scalar(
-                    result[:, 0, :], larger[:, :HALF],
-                    crowd_sb[:, 2 * k : 2 * k + 1], 0.0, ALU.mult, ALU.add,
+        v2 = [gather_exhibits(0, "h3_slot")]
+        x_c = [held([P, NP], U32, "x_c%d" % i) for i in range(2)]
+        x_s = [held([P, NP], U8, "x_s%d" % i) for i in range(2)]
+        for i in range(2):
+            nc.vector.quantize_mx(out=x_c[i][:].bitcast(FP8X4), scales=x_s[i][:], in_=x_bf[i][:])
+        v2.append(gather_exhibits(1, "x_bf1"))
+
+        tiles = S2 // P
+        for m in range(tiles):
+            e = []
+            for i in range(2):
+                acc = next_bank()
+                nc.tensor.matmul_mx(
+                    out=acc[:],
+                    lhsT=v2[m // 4][:, (m % 4) * P : (m % 4 + 1) * P].bitcast(FP8X4),
+                    lhsT_scale=v2_s[:, m * P : (m + 1) * P],
+                    rhs=x_c[i][:].bitcast(FP8X4), rhs_scale=x_s[i][:],
+                    start=True, stop=True,
                 )
-                nc.scalar.activation(
-                    result[:, 1, :], larger[:, HALF:], ACT.Copy, scale=crowd_sb[:, 2 * k + 1 : 2 * k + 2]
-                )
-                nc.sync.dma_start(
-                    out=out[2 * k * P : 2 * (k + 1) * P, n * HALF : (n + 1) * HALF].rearrange(
-                        "(r p) c -> p r c", p=P
-                    ),
-                    in_=result[:],
-                )
+                e.append(acc)
+            e1 = ring.tile([P, NP], F32, name="e1", bufs=4)
+            nc.scalar.copy(e1[:], e[0][:])
+            larger = ring.tile([P, NP], F32, name="larger")
+            nc.vector.tensor_tensor(larger[:], e[1][:], e1[:], ALU.max)
+            result = ring.tile([P, NP], F32, name="result", bufs=tiles)
+            factor = crowd_sb[:, m : m + 1]
+            if m == tiles - 1:
+                nc.vector.tensor_scalar(result[:, :HALF], larger[:, :HALF], factor, None, ALU.mult)
+                nc.scalar.activation(result[:, HALF:], larger[:, HALF:], ACT.Copy, scale=factor)
+            elif m % 3 == 2:
+                nc.scalar.activation(result[:], larger[:], ACT.Copy, scale=factor)
+            else:
+                nc.gpsimd.tensor_scalar(result[:], larger[:], factor, 0.0, ALU.mult, ALU.add)
+            nc.sync.dma_start(out=out[m * P : (m + 1) * P, :], in_=result[:])

@@ -19,9 +19,13 @@ ACT = mybir.ActivationFunctionType
 
 P = 128
 PACK = 4
-KP = P * PACK
+K_PASS = P * PACK
 BANK = 512
-HALF = 256
+BANKS = 8
+HALF = NP // 2
+BLOCKS = 16
+LIST_COLUMNS = BANK // 16
+SCALE_HOME = (16, 112)
 
 
 def tile_list_next_stop_proposer_kernel(
@@ -34,12 +38,15 @@ def tile_list_next_stop_proposer_kernel(
         keep = ctx.enter_context(tc.tile_pool(name="keep", bufs=1))
         ring = ctx.enter_context(tc.tile_pool(name="ring", bufs=3))
         psum = ctx.enter_context(tc.psum_pool(name="psum", bufs=1))
+
+        def bank(number):
+            return psum.tile([P, BANK], F32, name="bank%d" % number)
+
         taken = []
 
         def next_bank():
-            taken.append(psum.tile([P, BANK], F32, name="bank%d" % (len(taken) % 8)))
+            taken.append(bank(len(taken) % BANKS))
             return taken[-1]
-
 
         def held(shape, dtype, name, tag=None):
             return keep.tile(shape, dtype, name=name, tag=tag or name, align_bytes=64)
@@ -51,14 +58,15 @@ def tile_list_next_stop_proposer_kernel(
         warm = held([P, 2], F32, "warm")
         nc.vector.memset(warm[:, 0:1], 0.0)
         nc.scalar.activation(warm[:, 1:2], warm[:, 0:1], ACT.Sin)
+
         tab_s = held([P, T], U8, "tab_s")
         tab2_s = held([P, T3], U8, "tab2_s")
         w1_s_raw = held([P, 2, H], U8, "w1_s_raw")
         v_s = [held([P, S], U8, "v_s0")]
         nc.vector.memset(w1_s_raw[:].rearrange("p a c -> p (a c)").bitcast(I32), 0)
-        for rows in (slice(0, 16), slice(32, 64), slice(64, 112)):
-            nc.vector.memset(tab_s[rows, :].bitcast(I32), 0)
-        nc.vector.memset(tab2_s[0:112, :].bitcast(I32), 0)
+        for unused in (slice(0, SCALE_HOME[0]), slice(32, 64), slice(64, SCALE_HOME[1])):
+            nc.vector.memset(tab_s[unused, :].bitcast(I32), 0)
+        nc.vector.memset(tab2_s[0 : SCALE_HOME[1], :].bitcast(I32), 0)
         nc.vector.memset(v_s[0][:].bitcast(I32), 0)
 
         tab = [held([P, T], U32, "tab0")]
@@ -71,7 +79,7 @@ def tile_list_next_stop_proposer_kernel(
         def load_w(name, w, a):
             nc.sync.dma_start(
                 out=w_raw[name, a][:],
-                in_=w[a * KP : (a + 1) * KP, :].rearrange("(p j) c -> p j c", j=PACK),
+                in_=w[a * K_PASS : (a + 1) * K_PASS, :].rearrange("(p j) c -> p j c", j=PACK),
             )
 
         def load_words(dst, words, a):
@@ -81,15 +89,14 @@ def tile_list_next_stop_proposer_kernel(
             )
 
         nc.sync.dma_start(idx[:], offs)
-        scale_home = (16, 112)
         for a in range(2):
             nc.sync.dma_start(
-                out=tab_s[scale_home[a] : scale_home[a] + 16, :].bitcast(I32),
+                out=tab_s[SCALE_HOME[a] : SCALE_HOME[a] + BLOCKS, :].bitcast(I32),
                 in_=tab_scales[a].bitcast(I32),
             )
         load_w("w2", w2, 0)
         nc.sync.dma_start(idx2[:], offs2)
-        nc.sync.dma_start(out=tab2_s[112:128, :].bitcast(I32), in_=tab2_scales[0].bitcast(I32))
+        nc.sync.dma_start(out=tab2_s[SCALE_HOME[1] : P, :].bitcast(I32), in_=tab2_scales[0].bitcast(I32))
         nc.sync.dma_start(picks[0][:], pos1)
         nc.sync.dma_start(picks[1][:], pos2)
         load_w("w2", w2, 1)
@@ -98,10 +105,10 @@ def tile_list_next_stop_proposer_kernel(
         )
         nc.sync.dma_start(out=gain_sb[:], in_=gain.rearrange("(p t) -> p t", t=PACK))
         load_words(tab[0], tab_words, 0)
-        for q in range(4):
+        for quadrant in range(4):
             nc.gpsimd.dma_start(
-                out=w1_s_raw[32 * q : 32 * q + 4, :, :].bitcast(I32),
-                in_=w1_scales[:, 4 * q : 4 * q + 4, :].rearrange("a r c -> r a c").bitcast(I32),
+                out=w1_s_raw[32 * quadrant : 32 * quadrant + 4, :, :].bitcast(I32),
+                in_=w1_scales[:, 4 * quadrant : 4 * quadrant + 4, :].rearrange("a r c -> r a c").bitcast(I32),
             )
 
         v_s_rows = held([P, S], U8, "v_s_rows")
@@ -109,14 +116,14 @@ def tile_list_next_stop_proposer_kernel(
         w_raw["w3", 0] = held([P, PACK, H], F32, "w3_raw0", tag="tab_s")
         load_w("w3", w3, 0)
 
-        def move_scale_rows(plane, rows, first):
-            for q in range(4):
+        def move_scale_rows(plane, gathered, first):
+            for quadrant in range(4):
                 nc.sync.dma_start(
-                    out=plane[32 * q : 32 * q + 4, :].bitcast(I32),
-                    in_=rows[first + 4 * q : first + 4 * q + 4, :].bitcast(I32),
+                    out=plane[32 * quadrant : 32 * quadrant + 4, :].bitcast(I32),
+                    in_=gathered[first + 4 * quadrant : first + 4 * quadrant + 4, :].bitcast(I32),
                 )
 
-        move_scale_rows(v_s[0], v_s_rows, scale_home[0])
+        move_scale_rows(v_s[0], v_s_rows, SCALE_HOME[0])
         v2_s_rows = held([P, S2], U8, "v2_s_rows")
         nc.vector.tensor_copy(v2_s_rows[:], tab2_s[:].indirect(idx2[:]))
 
@@ -131,8 +138,8 @@ def tile_list_next_stop_proposer_kernel(
                 w_raw[name, a][:].rearrange("p j (m t) -> p m t j", t=PACK),
             )
 
-        def quantize_w(name, a, tag=None):
-            w_c[name, a] = held([P, H], U32, "%s_c%d" % (name, a), tag=tag)
+        def quantize_w(name, a):
+            w_c[name, a] = held([P, H], U32, "%s_c%d" % (name, a))
             w_s[name, a] = held([P, H], U8, "%s_s%d" % (name, a))
             nc.vector.quantize_mx(
                 out=w_c[name, a][:].bitcast(FP8X4), scales=w_s[name, a][:], in_=w_bf[name, a][:]
@@ -144,7 +151,7 @@ def tile_list_next_stop_proposer_kernel(
         quantize_w("w2", 0)
         v_s.append(held([P, S], U8, "v_s1", tag="w2_bf0"))
         nc.vector.memset(v_s[1][:].bitcast(I32), 0)
-        move_scale_rows(v_s[1], v_s_rows, scale_home[1])
+        move_scale_rows(v_s[1], v_s_rows, SCALE_HOME[1])
 
         interleave_w(nc.scalar.copy, "w2", 1)
         w_raw["w3", 1] = held([P, PACK, H], F32, "w3_raw1", tag="h0_slot")
@@ -169,12 +176,13 @@ def tile_list_next_stop_proposer_kernel(
         )
         v2_s = held([P, S2], U8, "v2_s", tag="w1_s_raw")
         nc.vector.memset(v2_s[:].bitcast(I32), 0)
-        move_scale_rows(v2_s, v2_s_rows, 112)
+        move_scale_rows(v2_s, v2_s_rows, SCALE_HOME[1])
         quantize_w("w3", 0)
 
         v1 = [held([P, BANK], U32, "v1_0", tag="w3_bf0"), held([P, BANK], U32, "v1_1")]
         for c in range(2):
-            nc.vector.tensor_copy(v1[c][:], tab[1][:].indirect(idx[:, 32 * c : 32 * (c + 1)]))
+            offsets = idx[:, c * LIST_COLUMNS : (c + 1) * LIST_COLUMNS]
+            nc.vector.tensor_copy(v1[c][:], tab[1][:].indirect(offsets))
         interleave_w(nc.vector.tensor_copy, "w3", 1, tag="tab1")
 
         def first_stage_product(name, t, c):
@@ -197,7 +205,7 @@ def tile_list_next_stop_proposer_kernel(
             return acc
 
         picked = [held([P, PACK, NP], F32, "picked%d" % i) for i in range(2)]
-        h_tags = {0: "h0_slot", 3: "h3_slot"}
+        h_tags = {0: "h0_slot", PACK - 1: "h3_slot"}
         h = {}
 
         def pick(i, t):
@@ -257,9 +265,10 @@ def tile_list_next_stop_proposer_kernel(
             pick(i, PACK - 1)
             interleave_x(i, 2)
 
-        def gather_exhibits(half, tag):
-            words = held([P, BANK], U32, "v2_%d" % half, tag=tag)
-            nc.vector.tensor_copy(words[:], tab2[:].indirect(idx2[:, 32 * half : 32 * (half + 1)]))
+        def gather_exhibits(part, tag):
+            words = held([P, BANK], U32, "v2_%d" % part, tag=tag)
+            offsets = idx2[:, part * LIST_COLUMNS : (part + 1) * LIST_COLUMNS]
+            nc.vector.tensor_copy(words[:], tab2[:].indirect(offsets))
             return words
 
         v2 = [gather_exhibits(0, "h3_slot")]
@@ -270,13 +279,20 @@ def tile_list_next_stop_proposer_kernel(
         v2.append(gather_exhibits(1, "x_bf1"))
 
         tiles = S2 // P
+        per_part = BANK // P
+
+        def second_stage_bank(i, m):
+            if m < per_part:
+                return bank(m % 2 if i == 0 else 2 + m)
+            return bank(m - 2 if i == 0 else (m + 2) % BANKS)
+
         for m in range(tiles):
             e = []
             for i in range(2):
-                acc = next_bank()
+                acc = second_stage_bank(i, m)
                 nc.tensor.matmul_mx(
                     out=acc[:],
-                    lhsT=v2[m // 4][:, (m % 4) * P : (m % 4 + 1) * P].bitcast(FP8X4),
+                    lhsT=v2[m // per_part][:, (m % per_part) * P : (m % per_part + 1) * P].bitcast(FP8X4),
                     lhsT_scale=v2_s[:, m * P : (m + 1) * P],
                     rhs=x_c[i][:].bitcast(FP8X4), rhs_scale=x_s[i][:],
                     start=True, stop=True,
@@ -288,11 +304,15 @@ def tile_list_next_stop_proposer_kernel(
             nc.vector.tensor_tensor(larger[:], e[1][:], e1[:], ALU.max)
             result = ring.tile([P, NP], F32, name="result", bufs=tiles)
             factor = crowd_sb[:, m : m + 1]
+            rows = out[m * P : (m + 1) * P, :]
             if m == tiles - 1:
                 nc.vector.tensor_scalar(result[:, :HALF], larger[:, :HALF], factor, None, ALU.mult)
+                nc.sync.dma_start(out=rows[:, :HALF], in_=result[:, :HALF])
                 nc.scalar.activation(result[:, HALF:], larger[:, HALF:], ACT.Copy, scale=factor)
-            elif m % 3 == 2:
+                nc.scalar.dma_start(out=rows[:, HALF:], in_=result[:, HALF:])
+                continue
+            if m % 3 == 2:
                 nc.scalar.activation(result[:], larger[:], ACT.Copy, scale=factor)
             else:
                 nc.gpsimd.tensor_scalar(result[:], larger[:], factor, 0.0, ALU.mult, ALU.add)
-            nc.sync.dma_start(out=out[m * P : (m + 1) * P, :], in_=result[:])
+            nc.sync.dma_start(out=rows, in_=result[:])

import math
from contextlib import ExitStack

import concourse.mybir as mybir

K, T, S, H, T3, S2, NP = 1024, 4096, 1024, 512, 2048, 1024, 512
FLOPS = 2 * (3 * K * H * S + 2 * H * S2 * NP)

F32 = mybir.dt.float32
BF16 = mybir.dt.bfloat16
I32 = mybir.dt.int32
U32 = mybir.dt.uint32
U16 = mybir.dt.uint16
U8 = mybir.dt.uint8
FP8X4 = mybir.dt.float8_e4m3fn_x4
FP4X4 = mybir.dt.float4_e2m1fn_x4
ALU = mybir.AluOpType
ACT = mybir.ActivationFunctionType

P = 128
PACK = 4
K_PASS = P * PACK
BANK = 512
BANKS = 8
HALF = NP // 2
BLOCKS = 16
LIST_COLUMNS = BANK // 16
SCALE_HOME = (16, 112)


def tile_list_next_stop_proposer_kernel(
    tc, tab_words, tab_scales, offs, tab2_words, tab2_scales, offs2, pos1, pos2,
    w1_words, w1_scales, w2, w3, gain, crowd, out,
):
    nc = tc.nc
    with ExitStack() as ctx:
        lists = ctx.enter_context(tc.tile_pool(name="lists", bufs=1))
        keep = ctx.enter_context(tc.tile_pool(name="keep", bufs=1))
        ring = ctx.enter_context(tc.tile_pool(name="ring", bufs=3))
        psum = ctx.enter_context(tc.psum_pool(name="psum", bufs=1))

        def bank(number):
            return psum.tile([P, BANK], F32, name="bank%d" % number)

        taken = []

        def next_bank():
            taken.append(bank(len(taken) % BANKS))
            return taken[-1]

        def held(shape, dtype, name, tag=None):
            return keep.tile(shape, dtype, name=name, tag=tag or name, align_bytes=64)

        idx = lists.tile([P, S // 16], U16, name="idx")
        idx2 = lists.tile([P, S2 // 16], U16, name="idx2")
        picks = [lists.tile([P, NP // 16], U16, name="pick%d" % i) for i in range(2)]

        warm = held([P, 2], F32, "warm")
        nc.vector.memset(warm[:, 0:1], 0.0)
        nc.scalar.activation(warm[:, 1:2], warm[:, 0:1], ACT.Sin)

        tab_s = held([P, T], U8, "tab_s")
        tab2_s = held([P, T3], U8, "tab2_s")
        w1_s_raw = held([P, 2, H], U8, "w1_s_raw")
        v_s = [held([P, S], U8, "v_s0")]
        nc.vector.memset(w1_s_raw[:].rearrange("p a c -> p (a c)").bitcast(I32), 0)
        for unused in (slice(0, SCALE_HOME[0]), slice(32, 64), slice(64, SCALE_HOME[1])):
            nc.vector.memset(tab_s[unused, :].bitcast(I32), 0)
        nc.vector.memset(tab2_s[0 : SCALE_HOME[1], :].bitcast(I32), 0)
        nc.vector.memset(v_s[0][:].bitcast(I32), 0)

        tab = [held([P, T], U32, "tab0")]
        w_raw = {}
        w_raw["w2", 0] = held([P, PACK, H], F32, "w2_raw0", tag="tab1")
        w_raw["w2", 1] = held([P, PACK, H], F32, "w2_raw1", tag="h0_slot")
        w1_raw = held([P, 2, 2 * H], U8, "w1_raw")
        gain_sb = held([P, PACK], F32, "gain_sb")

        def load_w(name, w, a):
            nc.sync.dma_start(
                out=w_raw[name, a][:],
                in_=w[a * K_PASS : (a + 1) * K_PASS, :].rearrange("(p j) c -> p j c", j=PACK),
            )

        def load_words(dst, words, a):
            nc.sync.dma_start(
                out=dst[:].bitcast(I32),
                in_=words[a].rearrange("p n t -> p (n t)").bitcast(I32),
            )

        nc.sync.dma_start(idx[:], offs)
        for a in range(2):
            nc.sync.dma_start(
                out=tab_s[SCALE_HOME[a] : SCALE_HOME[a] + BLOCKS, :].bitcast(I32),
                in_=tab_scales[a].bitcast(I32),
            )
        load_w("w2", w2, 0)
        nc.sync.dma_start(idx2[:], offs2)
        nc.sync.dma_start(out=tab2_s[SCALE_HOME[1] : P, :].bitcast(I32), in_=tab2_scales[0].bitcast(I32))
        nc.sync.dma_start(picks[0][:], pos1)
        nc.sync.dma_start(picks[1][:], pos2)
        load_w("w2", w2, 1)
        nc.sync.dma_start(
            out=w1_raw[:].bitcast(I32), in_=w1_words.rearrange("a p c -> p a c").bitcast(I32)
        )
        nc.sync.dma_start(out=gain_sb[:], in_=gain.rearrange("(p t) -> p t", t=PACK))
        load_words(tab[0], tab_words, 0)
        for quadrant in range(4):
            nc.gpsimd.dma_start(
                out=w1_s_raw[32 * quadrant : 32 * quadrant + 4, :, :].bitcast(I32),
                in_=w1_scales[:, 4 * quadrant : 4 * quadrant + 4, :].rearrange("a r c -> r a c").bitcast(I32),
            )

        v_s_rows = held([P, S], U8, "v_s_rows")
        nc.vector.tensor_copy(v_s_rows[:], tab_s[:].indirect(idx[:]))
        w_raw["w3", 0] = held([P, PACK, H], F32, "w3_raw0", tag="tab_s")
        load_w("w3", w3, 0)

        def move_scale_rows(plane, gathered, first):
            for quadrant in range(4):
                nc.sync.dma_start(
                    out=plane[32 * quadrant : 32 * quadrant + 4, :].bitcast(I32),
                    in_=gathered[first + 4 * quadrant : first + 4 * quadrant + 4, :].bitcast(I32),
                )

        move_scale_rows(v_s[0], v_s_rows, SCALE_HOME[0])
        v2_s_rows = held([P, S2], U8, "v2_s_rows")
        nc.vector.tensor_copy(v2_s_rows[:], tab2_s[:].indirect(idx2[:]))

        w_bf = {}
        w_c = {}
        w_s = {}

        def interleave_w(copy, name, a, tag=None):
            w_bf[name, a] = held([P, PACK * H], BF16, "%s_bf%d" % (name, a), tag=tag)
            copy(
                w_bf[name, a][:].rearrange("p (t m j) -> p m t j", t=PACK, j=PACK),
                w_raw[name, a][:].rearrange("p j (m t) -> p m t j", t=PACK),
            )

        def quantize_w(name, a):
            w_c[name, a] = held([P, H], U32, "%s_c%d" % (name, a))
            w_s[name, a] = held([P, H], U8, "%s_s%d" % (name, a))
            nc.vector.quantize_mx(
                out=w_c[name, a][:].bitcast(FP8X4), scales=w_s[name, a][:], in_=w_bf[name, a][:]
            )

        interleave_w(nc.scalar.copy, "w2", 0)
        tab.append(held([P, T], U32, "tab1"))
        load_words(tab[1], tab_words, 1)
        quantize_w("w2", 0)
        v_s.append(held([P, S], U8, "v_s1", tag="w2_bf0"))
        nc.vector.memset(v_s[1][:].bitcast(I32), 0)
        move_scale_rows(v_s[1], v_s_rows, SCALE_HOME[1])

        interleave_w(nc.scalar.copy, "w2", 1)
        w_raw["w3", 1] = held([P, PACK, H], F32, "w3_raw1", tag="h0_slot")
        load_w("w3", w3, 1)
        interleave_w(nc.scalar.copy, "w3", 0)
        tab2 = held([P, T3], U32, "tab2", tag="tab_s")
        load_words(tab2, tab2_words, 0)

        w1_c = held([P, 2, 2 * H], U8, "w1_c")
        nc.vector.tensor_copy(
            w1_c[:].bitcast(U16).rearrange("p a (t m) -> p a t m", t=PACK),
            w1_raw[:].bitcast(U16).rearrange("p a (m t) -> p a t m", t=PACK),
        )
        quantize_w("w2", 1)

        v0 = held([P, S], U32, "v0")
        nc.vector.tensor_copy(v0[:], tab[0][:].indirect(idx[:]))
        w1_s = held([P, 2, H], U8, "w1_s", tag="tab0")
        nc.vector.tensor_copy(
            w1_s[:].rearrange("p a (t m) -> p a t m", t=PACK),
            w1_s_raw[:].rearrange("p a (m t) -> p a t m", t=PACK),
        )
        v2_s = held([P, S2], U8, "v2_s", tag="w1_s_raw")
        nc.vector.memset(v2_s[:].bitcast(I32), 0)
        move_scale_rows(v2_s, v2_s_rows, SCALE_HOME[1])
        quantize_w("w3", 0)

        v1 = [held([P, BANK], U32, "v1_0", tag="w3_bf0"), held([P, BANK], U32, "v1_1")]
        for c in range(2):
            offsets = idx[:, c * LIST_COLUMNS : (c + 1) * LIST_COLUMNS]
            nc.vector.tensor_copy(v1[c][:], tab[1][:].indirect(offsets))
        interleave_w(nc.vector.tensor_copy, "w3", 1, tag="tab1")

        def first_stage_product(name, t, c):
            acc = next_bank()
            cols = slice(c * BANK, (c + 1) * BANK)
            rows = slice(t * P, (t + 1) * P)
            for a in range(2):
                if name == "w1":
                    lhsT = w1_c[:, a, 2 * t * P : 2 * (t + 1) * P].bitcast(FP4X4)
                    lhsT_scale = w1_s[:, a, rows]
                else:
                    lhsT = w_c[name, a][:, rows].bitcast(FP8X4)
                    lhsT_scale = w_s[name, a][:, rows]
                rhs = v0[:, cols] if a == 0 else v1[c][:]
                nc.tensor.matmul_mx(
                    out=acc[:], lhsT=lhsT, lhsT_scale=lhsT_scale,
                    rhs=rhs.bitcast(FP8X4), rhs_scale=v_s[a][:, cols],
                    start=(a == 0), stop=(a == 1),
                )
            return acc

        picked = [held([P, PACK, NP], F32, "picked%d" % i) for i in range(2)]
        h_tags = {0: "h0_slot", PACK - 1: "h3_slot"}
        h = {}

        def pick(i, t):
            nc.vector.tensor_copy(picked[i][:, t, :], h[t][:].indirect(picks[i][:]))

        def cosine_term(t, c):
            b = first_stage_product("w2", t, c)
            a_sum = first_stage_product("w1", t, c)
            if t < PACK - 1:
                b_abs = ring.tile([P, BANK], F32, name="b_abs")
            else:
                b_abs = held([P, BANK], F32, "b_abs_last%d" % c, tag="x_bf%d" % c)
            nc.scalar.activation(b_abs[:], b[:], ACT.Abs)
            cos_b = picked[c][:, (t - 1) % PACK, :]
            nc.scalar.activation(cos_b, b_abs[:], ACT.Sin, bias=math.pi / 2, scale=-1.0)
            nc.vector.scalar_tensor_tensor(
                out=h[t][:, c * BANK : (c + 1) * BANK], in0=cos_b, scalar=gain_sb[:, t : t + 1],
                in1=a_sum[:], op0=ALU.mult, op1=ALU.mult,
            )

        def add_third_product(t, c):
            d = first_stage_product("w3", t, c)
            part = h[t][:, c * BANK : (c + 1) * BANK]
            nc.vector.scalar_tensor_tensor(
                out=part, in0=d[:], scalar=gain_sb[:, t : t + 1], in1=part, op0=ALU.mult, op1=ALU.add
            )

        h[0] = held([P, S], F32, "h0", tag=h_tags[0])
        quantize_w("w3", 1)
        cosine_term(0, 0)
        cosine_term(0, 1)
        add_third_product(0, 0)
        add_third_product(0, 1)
        crowd_sb = held([P, S2 // P], F32, "crowd_sb", tag="tab1")
        with nc.allow_non_contiguous_dma(reason="one factor a partition for each tile of rows"):
            nc.sync.dma_start(out=crowd_sb[:], in_=crowd.rearrange("(i p) -> p i", p=P))
        for t in range(1, PACK):
            h[t] = held([P, S], F32, "h%d" % t, tag=h_tags.get(t))
            for c in range(2):
                cosine_term(t, c)
                pick(c, t - 1)
                add_third_product(t, c)

        x_bf = [held([P, PACK * NP], BF16, "x_bf%d" % i) for i in range(2)]

        def interleave_x(i, t0):
            dst = x_bf[i][:].rearrange("p (n t) -> p n t", t=PACK)[:, :, t0 : t0 + 2]
            src = picked[i][:, t0 : t0 + 2, :].rearrange("p t n -> p n t")
            if i == 0:
                nc.scalar.copy(dst, src)
            else:
                nc.scalar.activation(dst, src, ACT.Abs)

        for i in range(2):
            interleave_x(i, 0)
        for i in range(2):
            pick(i, PACK - 1)
            interleave_x(i, 2)

        def gather_exhibits(part, tag):
            words = held([P, BANK], U32, "v2_%d" % part, tag=tag)
            offsets = idx2[:, part * LIST_COLUMNS : (part + 1) * LIST_COLUMNS]
            nc.vector.tensor_copy(words[:], tab2[:].indirect(offsets))
            return words

        v2 = [gather_exhibits(0, "h3_slot")]
        x_c = [held([P, NP], U32, "x_c%d" % i) for i in range(2)]
        x_s = [held([P, NP], U8, "x_s%d" % i) for i in range(2)]
        for i in range(2):
            nc.vector.quantize_mx(out=x_c[i][:].bitcast(FP8X4), scales=x_s[i][:], in_=x_bf[i][:])
        v2.append(gather_exhibits(1, "x_bf1"))

        tiles = S2 // P
        per_part = BANK // P

        def second_stage_bank(i, m):
            if m < per_part:
                return bank(m % 2 if i == 0 else 2 + m)
            return bank(m - 2 if i == 0 else (m + 2) % BANKS)

        for m in range(tiles):
            e = []
            for i in range(2):
                acc = second_stage_bank(i, m)
                nc.tensor.matmul_mx(
                    out=acc[:],
                    lhsT=v2[m // per_part][:, (m % per_part) * P : (m % per_part + 1) * P].bitcast(FP8X4),
                    lhsT_scale=v2_s[:, m * P : (m + 1) * P],
                    rhs=x_c[i][:].bitcast(FP8X4), rhs_scale=x_s[i][:],
                    start=True, stop=True,
                )
                e.append(acc)
            e1 = ring.tile([P, NP], F32, name="e1", bufs=4)
            nc.scalar.copy(e1[:], e[0][:])
            larger = ring.tile([P, NP], F32, name="larger")
            nc.vector.tensor_tensor(larger[:], e[1][:], e1[:], ALU.max)
            result = ring.tile([P, NP], F32, name="result", bufs=tiles)
            factor = crowd_sb[:, m : m + 1]
            rows = out[m * P : (m + 1) * P, :]
            if m == tiles - 1:
                nc.vector.tensor_scalar(result[:, :HALF], larger[:, :HALF], factor, None, ALU.mult)
                nc.sync.dma_start(out=rows[:, :HALF], in_=result[:, :HALF])
                nc.scalar.activation(result[:, HALF:], larger[:, HALF:], ACT.Copy, scale=factor)
                nc.scalar.dma_start(out=rows[:, HALF:], in_=result[:, HALF:])
                continue
            if m % 3 == 2:
                nc.scalar.activation(result[:], larger[:], ACT.Copy, scale=factor)
            else:
                nc.gpsimd.tensor_scalar(result[:], larger[:], factor, 0.0, ALU.mult, ALU.add)
            nc.sync.dma_start(out=rows, in_=result[:])
